import numpy as np
import ml_dtypes


def mxq(x, axis, fmt="e4m3"):
    dtype, down = {"e4m3": (ml_dtypes.float8_e4m3fn, 7), "e5m2": (ml_dtypes.float8_e5m2, 14)}[fmt]
    v = np.moveaxis(np.asarray(x, np.float32).astype(ml_dtypes.bfloat16).astype(np.float64), axis, -1)
    blocks = v.reshape(v.shape[:-1] + (-1, 32))
    amax = np.abs(blocks).max(-1, keepdims=True)
    byte = np.maximum(np.where(amax > 0, np.frexp(amax)[1] - 1 + 127, 0) - down, 1)
    scale = np.exp2(byte - 127.0)
    codes = (blocks / scale).astype(np.float32).astype(dtype).astype(np.float64)
    return np.moveaxis((codes * scale).reshape(v.shape), -1, axis)


WIDE = False


def mx_kscale(k, group=512):
    if not WIDE:
        return np.ones(k)
    levels = np.array([10, -10, 5, -5, 0])
    if group != 512:
        return np.exp2(np.random.permutation(np.resize(levels, k // group))).repeat(group)
    if k % 512:
        return np.exp2(np.random.permutation(np.resize(levels, k // 32))).repeat(32)
    a = np.empty((k // 512, 16))
    for p in range(k // 512):
        a[p, :8] = np.random.permutation(np.resize(levels, 8))
        for g in range(8):
            far = levels[np.abs(levels - a[p, g]) >= 10]
            a[p, g + 8] = far[np.random.randint(len(far))]
    return np.exp2(a.ravel()).repeat(32)


def f64(x):
    return np.asarray(x).astype(np.float64)


E2M1 = np.array([0.0, 0.5, 1.0, 1.5, 2.0, 3.0, 4.0, 6.0, -0.0, -0.5, -1.0, -1.5, -2.0, -3.0, -4.0, -6.0])


def pack_group(w):
    k, n = w.shape
    w = f64(np.asarray(w, np.float32).astype(ml_dtypes.bfloat16)).reshape(k // 32, 32, n)
    amax = np.abs(w).max(1)
    mant, ex = np.frexp(amax / 6.0)
    byte = np.clip(np.where(amax > 0, np.where(mant > 0.5, ex, ex - 1) + 127, 1), 1, 254)
    scaled = (w * np.exp2(127.0 - byte)[:, None, :]).reshape(k, n).astype(np.float32)
    c = np.ascontiguousarray(scaled.reshape(k // 4, 4, n).transpose(0, 2, 1)).astype(ml_dtypes.float4_e2m1fn).view(np.uint8) & 0xF
    return np.ascontiguousarray((c[..., 0::2] | (c[..., 1::2] << 4)).reshape(k // 4, 2 * n)), byte.astype(np.uint8)


def unpack_group(words, scales):
    p, n = words.shape[0], scales.shape[1]
    words = np.ascontiguousarray(words).reshape(p, n, 2)
    nib = np.empty((p, n, 4), np.uint8)
    nib[..., 0::2] = words & 0xF
    nib[..., 1::2] = words >> 4
    return E2M1[nib].transpose(0, 2, 1).reshape(4 * p, n) * np.repeat(np.exp2(scales.astype(np.float64) - 127.0), 32, axis=0)


G, D, M, N = 4, 256, 256, 512


def setup_inputs():
    n = np.random.standard_normal
    s = mx_kscale(D, 0)[:, None]
    w_ = [pack_group(w) for w in n((G, D, M)) / np.sqrt(D) / s]
    return {
        "x": (n((G, D, N)) * s).astype(np.float32),
        "w_words": np.stack([w[0] for w in w_]),
        "w_scales": np.stack([w[1] for w in w_]),
        "b": (0.5 * n((G, M, 1))).astype(np.float32),
    }


def reference(x, w_words, w_scales, b):
    xq = mxq(f64(x), 1, "e4m3")
    y = np.stack([unpack_group(w_words[g], w_scales[g]) for g in range(G)]).transpose(0, 2, 1) @ xq
    y = y + f64(b)
    y = np.maximum(y, 0.0)
    return y

@@ -1,0 +1,157 @@
+from contextlib import ExitStack
+
+import concourse.mybir as mybir
+
+G, D, M, N = 4, 256, 256, 512
+FLOPS = 2 * G * D * M * N
+
+F32 = mybir.dt.float32
+BF16 = mybir.dt.bfloat16
+I32 = mybir.dt.int32
+U32 = mybir.dt.uint32
+U8 = mybir.dt.uint8
+FP8X4 = mybir.dt.float8_e4m3fn_x4
+FP4X4 = mybir.dt.float4_e2m1fn_x4
+ACT = mybir.ActivationFunctionType
+ALU = mybir.AluOpType
+
+P = 128
+PACK = 4
+ROWS = D // PACK
+SIDE = P // ROWS
+PAIRS = G // SIDE
+M_TILES = M // P
+QUAD = 32
+STEP = 256
+STEPS = PAIRS * (N // STEP)
+SCALAR_COLS = (96, 64, 0, 0)
+
+
+def tile_rows_glin_relu_bias_kernel(tc, x, w_words, w_scales, b, out):
+    nc = tc.nc
+    with ExitStack() as ctx:
+        keep = ctx.enter_context(tc.tile_pool(name="keep", bufs=1))
+        raw_pool = ctx.enter_context(tc.tile_pool(name="raw", bufs=4))
+        psum = ctx.enter_context(tc.psum_pool(name="psum", bufs=1))
+        ctx.enter_context(tc.manual_schedule())
+
+        w_tile = keep.tile([P, PAIRS, 2 * M], U8, align_bytes=64)
+        ws_tile = keep.tile([P, PAIRS, M], U8, align_bytes=64)
+        bias_rows = keep.tile([P, G * M_TILES * QUAD], F32, align_bytes=64)
+        bias_cols = keep.tile([P, G * M_TILES * QUAD], F32, align_bytes=64)
+        codes = keep.tile([P, (STEPS + 1) * STEP], U32, align_bytes=64)
+        scales = keep.tile([P, (STEPS + 1) * STEP], U8, align_bytes=64)
+        warm = keep.tile([P, 1], F32)
+        grouped = [keep.tile([P, STEP, PACK], BF16, name="grouped%d" % u, align_bytes=64) for u in range(STEPS)]
+        results = {
+            (u, h): keep.tile([P, SIDE, STEP], F32, name="result%d_%d" % (u, h))
+            for u in range(STEPS)
+            for h in range(M_TILES)
+        }
+        banks = {
+            (c, k): psum.tile([P, N], F32, name="bank%d_%d" % (c, k))
+            for c in range(SIDE)
+            for k in range(2 * M_TILES)
+        }
+
+        x_view = x.rearrange("(s c) (p j) n -> s (c p) j n", c=SIDE, j=PACK)
+        out_view = out.rearrange("(s c) (h m) n -> s h m c n", c=SIDE, m=P)
+
+        def columns(u):
+            n0 = (u % (N // STEP)) * STEP
+            return slice(n0, n0 + STEP)
+
+        raw = {}
+
+        def load(u):
+            raw[u] = raw_pool.tile([P, PACK, STEP], F32, name="raw")
+            nc.sync.dma_start(out=raw[u][:], in_=x_view[u // (N // STEP), :, :, columns(u)])
+
+        def interleave(u):
+            cut = STEP - SCALAR_COLS[u]
+            src = raw[u][:].rearrange("p t (c i) -> p c t i", i=4)
+            dst = grouped[u][:].rearrange("p (c i) t -> p c t i", i=4)
+            mid = STEP // 2
+            nc.vector.tensor_copy(out=dst[:, : mid // 4], in_=src[:, : mid // 4])
+            nc.vector.tensor_copy(out=dst[:, mid // 4 : cut // 4], in_=src[:, mid // 4 : cut // 4])
+            if cut < STEP:
+                nc.scalar.copy(out=dst[:, cut // 4 :], in_=src[:, cut // 4 :])
+
+        def quantize(u):
+            half = STEP // 2
+            for n0 in (0, half):
+                cols = slice((u + 1) * STEP + n0, (u + 1) * STEP + n0 + half)
+                nc.vector.quantize_mx(
+                    out=codes[:, cols].bitcast(FP8X4),
+                    scales=scales[:, cols],
+                    in_=grouped[u][:, n0 : n0 + half, :].rearrange("p n t -> p (n t)"),
+                )
+
+        def bank(u, h, c):
+            return banks[(c, (u % 2) * M_TILES + h)]
+
+        def multiply(u):
+            s = u // (N // STEP)
+            window = slice(u * STEP, u * STEP + N)
+            for h in range(M_TILES):
+                for c in range(SIDE):
+                    rows = slice(c * ROWS, (c + 1) * ROWS)
+                    nc.tensor.matmul_mx(
+                        out=bank(u, h, c)[:],
+                        lhsT=w_tile[rows, s, 2 * P * h : 2 * P * (h + 1)].bitcast(FP4X4),
+                        lhsT_scale=ws_tile[rows, s, P * h : P * (h + 1)],
+                        rhs=codes[rows, window].bitcast(FP8X4),
+                        rhs_scale=scales[rows, window],
+                        start=True,
+                        stop=True,
+                    )
+
+        def finish(u, h, c, on_vector):
+            g = (u // (N // STEP)) * SIDE + c
+            j = (g * M_TILES + h) * QUAD
+            bias = bias_cols[:, j : j + 1]
+            sums = bank(u, h, c)[:, N - STEP :]
+            dst = results[(u, h)][:, c, :]
+            if on_vector:
+                nc.vector.tensor_scalar(out=dst, in0=sums, scalar1=bias, scalar2=0.0, op0=ALU.add, op1=ALU.max)
+            else:
+                nc.scalar.activation(out=dst, in_=sums, func=ACT.Relu, bias=bias)
+
+        def store(u, h):
+            nc.sync.dma_start(out=out_view[u // (N // STEP), h, :, :, columns(u)], in_=results[(u, h)][:])
+
+        load(0)
+        nc.sync.dma_start(
+            out=w_tile[:].bitcast(I32),
+            in_=w_words.bitcast(I32).rearrange("(s c) p w -> (c p) s w", c=SIDE),
+        )
+        nc.vector.memset(bias_rows[:], 0.0)
+        nc.vector.memset(ws_tile[:].bitcast(I32), 0)
+        nc.vector.memset(codes[:, :STEP], 0)
+        nc.vector.memset(scales[:, :STEP].bitcast(I32), 0)
+        nc.scalar.dma_start(
+            out=bias_rows[0:P:QUAD, :].rearrange("q (j i) -> q j i", i=QUAD),
+            in_=b.rearrange("g (h q i) o -> q (g h) (i o)", h=M_TILES, i=QUAD),
+        )
+        ws_view = w_scales.bitcast(I32).rearrange("(s c) (k r) w -> r (c k) s w", c=SIDE, r=4)
+        for r in range(4):
+            nc.sync.dma_start(out=ws_tile[r:P:QUAD].bitcast(I32), in_=ws_view[r])
+        for u in range(1, STEPS):
+            load(u)
+        nc.scalar.activation(out=warm[:], in_=codes[:, 0:1].bitcast(F32), func=ACT.Relu)
+        nc.vector.transpose(out=bias_cols[:], in_=bias_rows[:])
+
+        def finish_step(u, shared):
+            for h in range(M_TILES):
+                finish(u, h, 0, False)
+                finish(u, h, 1, shared)
+                store(u, h)
+
+        for u in range(STEPS):
+            interleave(u)
+            if 1 <= u < STEPS - 1:
+                finish_step(u - 1, False)
+            quantize(u)
+            multiply(u)
+        finish_step(STEPS - 2, True)
+        finish_step(STEPS - 1, True)

@@ -22,26 +22,31 @@ SIDE = P // ROWS
 PAIRS = G // SIDE
 M_TILES = M // P
 QUAD = 32
+SCALE_ROWS = 4
+FP4_WORD_BYTES = 2
 STEP = 256
-STEPS = PAIRS * (N // STEP)
+STEPS_PER_PAIR = N // STEP
+STEPS = PAIRS * STEPS_PER_PAIR
+PIECE = STEP // 2
+RUN = 4
 SCALAR_COLS = (96, 64, 0, 0)
+SHARED_STEPS = 2
 
 
 def tile_rows_glin_relu_bias_kernel(tc, x, w_words, w_scales, b, out):
     nc = tc.nc
     with ExitStack() as ctx:
         keep = ctx.enter_context(tc.tile_pool(name="keep", bufs=1))
-        raw_pool = ctx.enter_context(tc.tile_pool(name="raw", bufs=4))
+        raw_pool = ctx.enter_context(tc.tile_pool(name="raw", bufs=STEPS))
         psum = ctx.enter_context(tc.psum_pool(name="psum", bufs=1))
         ctx.enter_context(tc.manual_schedule())
 
-        w_tile = keep.tile([P, PAIRS, 2 * M], U8, align_bytes=64)
+        w_tile = keep.tile([P, PAIRS, FP4_WORD_BYTES * M], U8, align_bytes=64)
         ws_tile = keep.tile([P, PAIRS, M], U8, align_bytes=64)
         bias_rows = keep.tile([P, G * M_TILES * QUAD], F32, align_bytes=64)
         bias_cols = keep.tile([P, G * M_TILES * QUAD], F32, align_bytes=64)
         codes = keep.tile([P, (STEPS + 1) * STEP], U32, align_bytes=64)
         scales = keep.tile([P, (STEPS + 1) * STEP], U8, align_bytes=64)
-        warm = keep.tile([P, 1], F32)
         grouped = [keep.tile([P, STEP, PACK], BF16, name="grouped%d" % u, align_bytes=64) for u in range(STEPS)]
         results = {
             (u, h): keep.tile([P, SIDE, STEP], F32, name="result%d_%d" % (u, h))
@@ -54,62 +59,61 @@ def tile_rows_glin_relu_bias_kernel(tc, x, w_words, w_scales, b, out):
             for k in range(2 * M_TILES)
         }
 
-        x_view = x.rearrange("(s c) (p j) n -> s (c p) j n", c=SIDE, j=PACK)
+        x_view = x.rearrange("(s c) (p t) n -> s (c p) t n", c=SIDE, t=PACK)
         out_view = out.rearrange("(s c) (h m) n -> s h m c n", c=SIDE, m=P)
-
-        def columns(u):
-            n0 = (u % (N // STEP)) * STEP
-            return slice(n0, n0 + STEP)
-
         raw = {}
 
-        def load(u):
-            raw[u] = raw_pool.tile([P, PACK, STEP], F32, name="raw")
-            nc.sync.dma_start(out=raw[u][:], in_=x_view[u // (N // STEP), :, :, columns(u)])
+        def pair(u):
+            return u // STEPS_PER_PAIR
 
-        def interleave(u):
-            cut = STEP - SCALAR_COLS[u]
-            src = raw[u][:].rearrange("p t (c i) -> p c t i", i=4)
-            dst = grouped[u][:].rearrange("p (c i) t -> p c t i", i=4)
-            mid = STEP // 2
-            nc.vector.tensor_copy(out=dst[:, : mid // 4], in_=src[:, : mid // 4])
-            nc.vector.tensor_copy(out=dst[:, mid // 4 : cut // 4], in_=src[:, mid // 4 : cut // 4])
-            if cut < STEP:
-                nc.scalar.copy(out=dst[:, cut // 4 :], in_=src[:, cut // 4 :])
-
-        def quantize(u):
-            half = STEP // 2
-            for n0 in (0, half):
-                cols = slice((u + 1) * STEP + n0, (u + 1) * STEP + n0 + half)
-                nc.vector.quantize_mx(
-                    out=codes[:, cols].bitcast(FP8X4),
-                    scales=scales[:, cols],
-                    in_=grouped[u][:, n0 : n0 + half, :].rearrange("p n t -> p (n t)"),
-                )
+        def columns(u):
+            n0 = (u % STEPS_PER_PAIR) * STEP
+            return slice(n0, n0 + STEP)
 
         def bank(u, h, c):
             return banks[(c, (u % 2) * M_TILES + h)]
 
+        def load(u):
+            raw[u] = raw_pool.tile([P, PACK, STEP], F32, name="raw")
+            nc.sync.dma_start(out=raw[u][:], in_=x_view[pair(u), :, :, columns(u)])
+
+        def interleave(u):
+            cut = (STEP - SCALAR_COLS[u]) // RUN
+            src = raw[u][:].rearrange("p t (r i) -> p r t i", i=RUN)
+            dst = grouped[u][:].rearrange("p (r i) t -> p r t i", i=RUN)
+            nc.vector.tensor_copy(out=dst[:, : PIECE // RUN], in_=src[:, : PIECE // RUN])
+            nc.vector.tensor_copy(out=dst[:, PIECE // RUN : cut], in_=src[:, PIECE // RUN : cut])
+            if SCALAR_COLS[u]:
+                nc.scalar.copy(out=dst[:, cut:], in_=src[:, cut:])
+
+        def quantize(u):
+            for n0 in range(0, STEP, PIECE):
+                cols = slice((u + 1) * STEP + n0, (u + 1) * STEP + n0 + PIECE)
+                nc.vector.quantize_mx(
+                    out=codes[:, cols].bitcast(FP8X4),
+                    scales=scales[:, cols],
+                    in_=grouped[u][:, n0 : n0 + PIECE, :].rearrange("p n t -> p (n t)"),
+                )
+
         def multiply(u):
-            s = u // (N // STEP)
             window = slice(u * STEP, u * STEP + N)
             for h in range(M_TILES):
                 for c in range(SIDE):
                     rows = slice(c * ROWS, (c + 1) * ROWS)
+                    words = slice(FP4_WORD_BYTES * P * h, FP4_WORD_BYTES * P * (h + 1))
                     nc.tensor.matmul_mx(
                         out=bank(u, h, c)[:],
-                        lhsT=w_tile[rows, s, 2 * P * h : 2 * P * (h + 1)].bitcast(FP4X4),
-                        lhsT_scale=ws_tile[rows, s, P * h : P * (h + 1)],
+                        lhsT=w_tile[rows, pair(u), words].bitcast(FP4X4),
+                        lhsT_scale=ws_tile[rows, pair(u), P * h : P * (h + 1)],
                         rhs=codes[rows, window].bitcast(FP8X4),
                         rhs_scale=scales[rows, window],
                         start=True,
                         stop=True,
                     )
 
-        def finish(u, h, c, on_vector):
-            g = (u // (N // STEP)) * SIDE + c
-            j = (g * M_TILES + h) * QUAD
-            bias = bias_cols[:, j : j + 1]
+        def read_out(u, h, c, on_vector):
+            col = ((pair(u) * SIDE + c) * M_TILES + h) * QUAD
+            bias = bias_cols[:, col : col + 1]
             sums = bank(u, h, c)[:, N - STEP :]
             dst = results[(u, h)][:, c, :]
             if on_vector:
@@ -117,8 +121,11 @@ def tile_rows_glin_relu_bias_kernel(tc, x, w_words, w_scales, b, out):
             else:
                 nc.scalar.activation(out=dst, in_=sums, func=ACT.Relu, bias=bias)
 
-        def store(u, h):
-            nc.sync.dma_start(out=out_view[u // (N // STEP), h, :, :, columns(u)], in_=results[(u, h)][:])
+        def finish(u):
+            for h in range(M_TILES):
+                read_out(u, h, 0, False)
+                read_out(u, h, 1, u >= STEPS - SHARED_STEPS)
+                nc.sync.dma_start(out=out_view[pair(u), h, :, :, columns(u)], in_=results[(u, h)][:])
 
         load(0)
         nc.sync.dma_start(
@@ -133,25 +140,18 @@ def tile_rows_glin_relu_bias_kernel(tc, x, w_words, w_scales, b, out):
             out=bias_rows[0:P:QUAD, :].rearrange("q (j i) -> q j i", i=QUAD),
             in_=b.rearrange("g (h q i) o -> q (g h) (i o)", h=M_TILES, i=QUAD),
         )
-        ws_view = w_scales.bitcast(I32).rearrange("(s c) (k r) w -> r (c k) s w", c=SIDE, r=4)
-        for r in range(4):
+        ws_view = w_scales.bitcast(I32).rearrange("(s c) (k r) w -> r (c k) s w", c=SIDE, r=SCALE_ROWS)
+        for r in range(SCALE_ROWS):
             nc.sync.dma_start(out=ws_tile[r:P:QUAD].bitcast(I32), in_=ws_view[r])
         for u in range(1, STEPS):
             load(u)
-        nc.scalar.activation(out=warm[:], in_=codes[:, 0:1].bitcast(F32), func=ACT.Relu)
         nc.vector.transpose(out=bias_cols[:], in_=bias_rows[:])
-
-        def finish_step(u, shared):
-            for h in range(M_TILES):
-                finish(u, h, 0, False)
-                finish(u, h, 1, shared)
-                store(u, h)
 
         for u in range(STEPS):
             interleave(u)
-            if 1 <= u < STEPS - 1:
-                finish_step(u - 1, False)
+            if 1 <= u <= STEPS - SHARED_STEPS:
+                finish(u - 1)
             quantize(u)
             multiply(u)
-        finish_step(STEPS - 2, True)
-        finish_step(STEPS - 1, True)
+        for u in range(STEPS - SHARED_STEPS, STEPS):
+            finish(u)

@@ -29,15 +29,13 @@ STEPS_PER_PAIR = N // STEP
 STEPS = PAIRS * STEPS_PER_PAIR
 PIECE = STEP // 2
 RUN = 4
-SCALAR_COLS = (96, 64, 0, 0)
-SHARED_STEPS = 2
+LEAD = 256
 
 
 def tile_rows_glin_relu_bias_kernel(tc, x, w_words, w_scales, b, out):
     nc = tc.nc
     with ExitStack() as ctx:
         keep = ctx.enter_context(tc.tile_pool(name="keep", bufs=1))
-        raw_pool = ctx.enter_context(tc.tile_pool(name="raw", bufs=STEPS))
         psum = ctx.enter_context(tc.psum_pool(name="psum", bufs=1))
         ctx.enter_context(tc.manual_schedule())
 
@@ -45,14 +43,9 @@ def tile_rows_glin_relu_bias_kernel(tc, x, w_words, w_scales, b, out):
         ws_tile = keep.tile([P, PAIRS, M], U8, align_bytes=64)
         bias_rows = keep.tile([P, G * M_TILES * QUAD], F32, align_bytes=64)
         bias_cols = keep.tile([P, G * M_TILES * QUAD], F32, align_bytes=64)
-        codes = keep.tile([P, (STEPS + 1) * STEP], U32, align_bytes=64)
-        scales = keep.tile([P, (STEPS + 1) * STEP], U8, align_bytes=64)
-        grouped = [keep.tile([P, STEP, PACK], BF16, name="grouped%d" % u, align_bytes=64) for u in range(STEPS)]
-        results = {
-            (u, h): keep.tile([P, SIDE, STEP], F32, name="result%d_%d" % (u, h))
-            for u in range(STEPS)
-            for h in range(M_TILES)
-        }
+        codes = keep.tile([P, LEAD + PAIRS * N], U32, align_bytes=64)
+        scales = keep.tile([P, LEAD + PAIRS * N], U8, align_bytes=64)
+        grouped = [keep.tile([P, N * PACK], BF16, name="grouped%d" % s, align_bytes=64) for s in range(PAIRS)]
         banks = {
             (c, k): psum.tile([P, N], F32, name="bank%d_%d" % (c, k))
             for c in range(SIDE)
@@ -61,97 +54,138 @@ def tile_rows_glin_relu_bias_kernel(tc, x, w_words, w_scales, b, out):
 
         x_view = x.rearrange("(s c) (p t) n -> s (c p) t n", c=SIDE, t=PACK)
         out_view = out.rearrange("(s c) (h m) n -> s h m c n", c=SIDE, m=P)
-        raw = {}
+        raw = []
+        results = {}
 
-        def pair(u):
-            return u // STEPS_PER_PAIR
+        def load(s, n0, n1, queue=nc.sync):
+            tile = keep.tile([P, PACK, n1 - n0], F32, name="raw%d_%d" % (s, n0))
+            raw.append((s, n0, n1, tile))
+            queue.dma_start(out=tile[:], in_=x_view[s, :, :, n0:n1])
 
-        def columns(u):
-            n0 = (u % STEPS_PER_PAIR) * STEP
-            return slice(n0, n0 + STEP)
+        def interleave(on_vector, s, n0, n1):
+            base, tile = [(a, t) for (r, a, e, t) in raw if r == s and a <= n0 and n1 <= e][0]
+            src = tile[:, :, n0 - base : n1 - base].rearrange("p t (r i) -> p r t i", i=RUN)
+            dst = grouped[s][:, PACK * n0 : PACK * n1].rearrange("p (r i t) -> p r t i", i=RUN, t=PACK)
+            if on_vector:
+                nc.vector.tensor_copy(out=dst, in_=src)
+            else:
+                nc.scalar.copy(out=dst, in_=src)
 
-        def bank(u, h, c):
-            return banks[(c, (u % 2) * M_TILES + h)]
+        def quantize(s, n0, n1):
+            cols = slice(LEAD + s * N + n0, LEAD + s * N + n1)
+            nc.vector.quantize_mx(
+                out=codes[:, cols].bitcast(FP8X4),
+                scales=scales[:, cols],
+                in_=grouped[s][:, PACK * n0 : PACK * n1],
+            )
 
-        def load(u):
-            raw[u] = raw_pool.tile([P, PACK, STEP], F32, name="raw")
-            nc.sync.dma_start(out=raw[u][:], in_=x_view[pair(u), :, :, columns(u)])
-
-        def interleave(u):
-            cut = (STEP - SCALAR_COLS[u]) // RUN
-            src = raw[u][:].rearrange("p t (r i) -> p r t i", i=RUN)
-            dst = grouped[u][:].rearrange("p (r i) t -> p r t i", i=RUN)
-            nc.vector.tensor_copy(out=dst[:, : PIECE // RUN], in_=src[:, : PIECE // RUN])
-            nc.vector.tensor_copy(out=dst[:, PIECE // RUN : cut], in_=src[:, PIECE // RUN : cut])
-            if SCALAR_COLS[u]:
-                nc.scalar.copy(out=dst[:, cut:], in_=src[:, cut:])
-
-        def quantize(u):
-            for n0 in range(0, STEP, PIECE):
-                cols = slice((u + 1) * STEP + n0, (u + 1) * STEP + n0 + PIECE)
-                nc.vector.quantize_mx(
-                    out=codes[:, cols].bitcast(FP8X4),
-                    scales=scales[:, cols],
-                    in_=grouped[u][:, n0 : n0 + PIECE, :].rearrange("p n t -> p (n t)"),
+        def multiply(s, h, end, k):
+            window = slice(LEAD + s * N + end - N, LEAD + s * N + end)
+            for c in range(SIDE):
+                rows = slice(c * ROWS, (c + 1) * ROWS)
+                words = slice(FP4_WORD_BYTES * P * h, FP4_WORD_BYTES * P * (h + 1))
+                nc.tensor.matmul_mx(
+                    out=banks[(c, k)][:],
+                    lhsT=w_tile[rows, s, words].bitcast(FP4X4),
+                    lhsT_scale=ws_tile[rows, s, P * h : P * (h + 1)],
+                    rhs=codes[rows, window].bitcast(FP8X4),
+                    rhs_scale=scales[rows, window],
+                    start=True,
+                    stop=True,
                 )
 
-        def multiply(u):
-            window = slice(u * STEP, u * STEP + N)
-            for h in range(M_TILES):
-                for c in range(SIDE):
-                    rows = slice(c * ROWS, (c + 1) * ROWS)
-                    words = slice(FP4_WORD_BYTES * P * h, FP4_WORD_BYTES * P * (h + 1))
-                    nc.tensor.matmul_mx(
-                        out=bank(u, h, c)[:],
-                        lhsT=w_tile[rows, pair(u), words].bitcast(FP4X4),
-                        lhsT_scale=ws_tile[rows, pair(u), P * h : P * (h + 1)],
-                        rhs=codes[rows, window].bitcast(FP8X4),
-                        rhs_scale=scales[rows, window],
-                        start=True,
-                        stop=True,
-                    )
-
-        def read_out(u, h, c, on_vector):
-            col = ((pair(u) * SIDE + c) * M_TILES + h) * QUAD
+        def read_out(on_vector, s, h, c, n0, end, k):
+            if (s, h, n0) not in results:
+                results[(s, h, n0)] = keep.tile([P, SIDE, end - n0], F32, name="result%d_%d_%d" % (s, h, n0))
+            col = ((s * SIDE + c) * M_TILES + h) * QUAD
             bias = bias_cols[:, col : col + 1]
-            sums = bank(u, h, c)[:, N - STEP :]
-            dst = results[(u, h)][:, c, :]
+            sums = banks[(c, k)][:, N - (end - n0) :]
+            dst = results[(s, h, n0)][:, c, :]
             if on_vector:
                 nc.vector.tensor_scalar(out=dst, in0=sums, scalar1=bias, scalar2=0.0, op0=ALU.add, op1=ALU.max)
             else:
                 nc.scalar.activation(out=dst, in_=sums, func=ACT.Relu, bias=bias)
 
-        def finish(u):
-            for h in range(M_TILES):
-                read_out(u, h, 0, False)
-                read_out(u, h, 1, u >= STEPS - SHARED_STEPS)
-                nc.sync.dma_start(out=out_view[pair(u), h, :, :, columns(u)], in_=results[(u, h)][:])
+        def store(s, h, n0, end, c=None, queue=nc.sync):
+            if c is None:
+                queue.dma_start(out=out_view[s, h, :, :, n0:end], in_=results[(s, h, n0)][:])
+            else:
+                queue.dma_start(out=out_view[s, h, :, c, n0:end], in_=results[(s, h, n0)][:, c, :])
 
-        load(0)
-        nc.sync.dma_start(
-            out=w_tile[:].bitcast(I32),
-            in_=w_words.bitcast(I32).rearrange("(s c) p w -> (c p) s w", c=SIDE),
-        )
-        nc.vector.memset(bias_rows[:], 0.0)
-        nc.vector.memset(ws_tile[:].bitcast(I32), 0)
-        nc.vector.memset(codes[:, :STEP], 0)
-        nc.vector.memset(scales[:, :STEP].bitcast(I32), 0)
-        nc.scalar.dma_start(
-            out=bias_rows[0:P:QUAD, :].rearrange("q (j i) -> q j i", i=QUAD),
-            in_=b.rearrange("g (h q i) o -> q (g h) (i o)", h=M_TILES, i=QUAD),
-        )
-        ws_view = w_scales.bitcast(I32).rearrange("(s c) (k r) w -> r (c k) s w", c=SIDE, r=SCALE_ROWS)
-        for r in range(SCALE_ROWS):
-            nc.sync.dma_start(out=ws_tile[r:P:QUAD].bitcast(I32), in_=ws_view[r])
-        for u in range(1, STEPS):
-            load(u)
-        nc.vector.transpose(out=bias_cols[:], in_=bias_rows[:])
+        def finish(s, h, n0, end, k, shared, apart=False):
+            read_out(False, s, h, 0, n0, end, k)
+            if apart:
+                store(s, h, n0, end, 0)
+            read_out(shared, s, h, 1, n0, end, k)
+            store(s, h, n0, end, 1 if apart else None)
 
-        for u in range(STEPS):
-            interleave(u)
-            if 1 <= u <= STEPS - SHARED_STEPS:
-                finish(u - 1)
-            quantize(u)
-            multiply(u)
-        for u in range(STEPS - SHARED_STEPS, STEPS):
-            finish(u)
+        def load_weights():
+            nc.sync.dma_start(
+                out=w_tile[:].bitcast(I32),
+                in_=w_words.bitcast(I32).rearrange("(s c) p w -> (c p) s w", c=SIDE),
+            )
+
+        def zero():
+            nc.vector.memset(bias_rows[:], 0.0)
+            nc.vector.memset(ws_tile[:].bitcast(I32), 0)
+            nc.vector.memset(codes[:, :LEAD], 0)
+            nc.vector.memset(scales[:, :LEAD].bitcast(I32), 0)
+
+        def load_bias(queue):
+            queue.dma_start(
+                out=bias_rows[0:P:QUAD, :].rearrange("q (j i) -> q j i", i=QUAD),
+                in_=b.rearrange("g (h q i) o -> q (g h) (i o)", h=M_TILES, i=QUAD),
+            )
+
+        def load_scales(queue, mix=False):
+            ws_view = w_scales.bitcast(I32).rearrange("(s c) (k r) w -> r (c k) s w", c=SIDE, r=SCALE_ROWS)
+            for r in range(SCALE_ROWS):
+                (nc.gpsimd if mix and r == 0 else queue).dma_start(out=ws_tile[r:P:QUAD].bitcast(I32), in_=ws_view[r])
+
+        def turn_bias():
+            nc.vector.transpose(out=bias_cols[:], in_=bias_rows[:])
+
+        V, S = True, False
+        load_weights()
+        load(0, 0, 256)
+        zero()
+        load_bias(nc.scalar)
+        load_scales(nc.sync)
+        load(0, 256, 512)
+        load(1, 0, 256)
+        load(1, 256, 512)
+        interleave(V, 0, 0, 128)
+        interleave(V, 0, 128, 160)
+        interleave(S, 0, 160, 256)
+        quantize(0, 0, 128)
+        quantize(0, 128, 256)
+        multiply(0, 0, 256, 0)
+        turn_bias()
+        multiply(0, 1, 256, 1)
+        interleave(V, 0, 256, 384)
+        interleave(V, 0, 384, 448)
+        interleave(S, 0, 448, 512)
+        finish(0, 0, 0, 256, 0, False)
+        finish(0, 1, 0, 256, 1, False)
+        quantize(0, 256, 384)
+        quantize(0, 384, 512)
+        multiply(0, 0, 512, 2)
+        multiply(0, 1, 512, 3)
+        interleave(V, 1, 0, 128)
+        interleave(V, 1, 128, 256)
+        finish(0, 0, 256, 512, 2, False)
+        finish(0, 1, 256, 512, 3, False)
+        quantize(1, 0, 128)
+        quantize(1, 128, 256)
+        multiply(1, 0, 256, 0)
+        multiply(1, 1, 256, 1)
+        interleave(V, 1, 256, 384)
+        interleave(V, 1, 384, 512)
+        quantize(1, 256, 384)
+        quantize(1, 384, 512)
+        multiply(1, 0, 512, 2)
+        multiply(1, 1, 512, 3)
+        finish(1, 0, 0, 256, 0, True)
+        finish(1, 1, 0, 256, 1, True)
+        finish(1, 0, 256, 512, 2, True)
+        finish(1, 1, 256, 512, 3, True)

@@ -27,25 +27,33 @@ FP4_WORD_BYTES = 2
 STEP = 256
 STEPS_PER_PAIR = N // STEP
 STEPS = PAIRS * STEPS_PER_PAIR
-PIECE = STEP // 2
+PIECES = 2
+PIECE = STEP // PIECES
 RUN = 4
-LEAD = 256
+SCALAR_COLS = ((40, 40), (0, 64), (0, 0), (0, 0))
+SHARED_STEPS = 2
 
 
 def tile_rows_glin_relu_bias_kernel(tc, x, w_words, w_scales, b, out):
     nc = tc.nc
     with ExitStack() as ctx:
         keep = ctx.enter_context(tc.tile_pool(name="keep", bufs=1))
+        raw_pool = ctx.enter_context(tc.tile_pool(name="raw", bufs=STEPS))
         psum = ctx.enter_context(tc.psum_pool(name="psum", bufs=1))
         ctx.enter_context(tc.manual_schedule())
 
-        w_tile = keep.tile([P, PAIRS, FP4_WORD_BYTES * M], U8, align_bytes=64)
+        w_tiles = [keep.tile([P, FP4_WORD_BYTES * M], U8, name="w%d" % s, align_bytes=64) for s in range(PAIRS)]
         ws_tile = keep.tile([P, PAIRS, M], U8, align_bytes=64)
         bias_rows = keep.tile([P, G * M_TILES * QUAD], F32, align_bytes=64)
         bias_cols = keep.tile([P, G * M_TILES * QUAD], F32, align_bytes=64)
-        codes = keep.tile([P, LEAD + PAIRS * N], U32, align_bytes=64)
-        scales = keep.tile([P, LEAD + PAIRS * N], U8, align_bytes=64)
-        grouped = [keep.tile([P, N * PACK], BF16, name="grouped%d" % s, align_bytes=64) for s in range(PAIRS)]
+        codes = keep.tile([P, (STEPS + 1) * STEP], U32, align_bytes=64)
+        scales = keep.tile([P, (STEPS + 1) * STEP], U8, align_bytes=64)
+        grouped = [keep.tile([P, STEP, PACK], BF16, name="grouped%d" % u, align_bytes=64) for u in range(STEPS)]
+        results = {
+            (u, h): keep.tile([P, SIDE, STEP], F32, name="result%d_%d" % (u, h))
+            for u in range(STEPS)
+            for h in range(M_TILES)
+        }
         banks = {
             (c, k): psum.tile([P, N], F32, name="bank%d_%d" % (c, k))
             for c in range(SIDE)
@@ -54,138 +62,108 @@ def tile_rows_glin_relu_bias_kernel(tc, x, w_words, w_scales, b, out):
 
         x_view = x.rearrange("(s c) (p t) n -> s (c p) t n", c=SIDE, t=PACK)
         out_view = out.rearrange("(s c) (h m) n -> s h m c n", c=SIDE, m=P)
-        raw = []
-        results = {}
+        w_view = w_words.bitcast(I32).rearrange("(s c) p w -> s (c p) w", c=SIDE)
+        ws_view = w_scales.bitcast(I32).rearrange("(s c) (k r) w -> r (c k) s w", c=SIDE, r=SCALE_ROWS)
+        raw = {}
 
-        def load(s, n0, n1, queue=nc.sync):
-            tile = keep.tile([P, PACK, n1 - n0], F32, name="raw%d_%d" % (s, n0))
-            raw.append((s, n0, n1, tile))
-            queue.dma_start(out=tile[:], in_=x_view[s, :, :, n0:n1])
+        def pair(u):
+            return u // STEPS_PER_PAIR
 
-        def interleave(on_vector, s, n0, n1):
-            base, tile = [(a, t) for (r, a, e, t) in raw if r == s and a <= n0 and n1 <= e][0]
-            src = tile[:, :, n0 - base : n1 - base].rearrange("p t (r i) -> p r t i", i=RUN)
-            dst = grouped[s][:, PACK * n0 : PACK * n1].rearrange("p (r i t) -> p r t i", i=RUN, t=PACK)
-            if on_vector:
-                nc.vector.tensor_copy(out=dst, in_=src)
-            else:
-                nc.scalar.copy(out=dst, in_=src)
+        def columns(u):
+            n0 = (u % STEPS_PER_PAIR) * STEP
+            return slice(n0, n0 + STEP)
 
-        def quantize(s, n0, n1):
-            cols = slice(LEAD + s * N + n0, LEAD + s * N + n1)
-            nc.vector.quantize_mx(
-                out=codes[:, cols].bitcast(FP8X4),
-                scales=scales[:, cols],
-                in_=grouped[s][:, PACK * n0 : PACK * n1],
-            )
+        def bank(u, h, c):
+            return banks[(c, (u % 2) * M_TILES + h)]
 
-        def multiply(s, h, end, k):
-            window = slice(LEAD + s * N + end - N, LEAD + s * N + end)
-            for c in range(SIDE):
-                rows = slice(c * ROWS, (c + 1) * ROWS)
-                words = slice(FP4_WORD_BYTES * P * h, FP4_WORD_BYTES * P * (h + 1))
-                nc.tensor.matmul_mx(
-                    out=banks[(c, k)][:],
-                    lhsT=w_tile[rows, s, words].bitcast(FP4X4),
-                    lhsT_scale=ws_tile[rows, s, P * h : P * (h + 1)],
-                    rhs=codes[rows, window].bitcast(FP8X4),
-                    rhs_scale=scales[rows, window],
-                    start=True,
-                    stop=True,
+        def load(u):
+            raw[u] = raw_pool.tile([P, PACK, STEP], F32, name="raw")
+            nc.sync.dma_start(out=raw[u][:], in_=x_view[pair(u), :, :, columns(u)])
+
+        def load_weights(s):
+            nc.sync.dma_start(out=w_tiles[s][:].bitcast(I32), in_=w_view[s])
+
+        def interleave(u):
+            src = raw[u][:].rearrange("p t (r i) -> p r t i", i=RUN)
+            dst = grouped[u][:].rearrange("p (r i) t -> p r t i", i=RUN)
+            for j, scalar_cols in enumerate(SCALAR_COLS[u]):
+                start, end = j * PIECE // RUN, (j + 1) * PIECE // RUN
+                cut = end - scalar_cols // RUN
+                nc.vector.tensor_copy(out=dst[:, start:cut], in_=src[:, start:cut])
+                if scalar_cols:
+                    nc.scalar.copy(out=dst[:, cut:end], in_=src[:, cut:end])
+
+        def quantize(u):
+            for n0 in range(0, STEP, PIECE):
+                cols = slice((u + 1) * STEP + n0, (u + 1) * STEP + n0 + PIECE)
+                nc.vector.quantize_mx(
+                    out=codes[:, cols].bitcast(FP8X4),
+                    scales=scales[:, cols],
+                    in_=grouped[u][:, n0 : n0 + PIECE, :].rearrange("p n t -> p (n t)"),
                 )
 
-        def read_out(on_vector, s, h, c, n0, end, k):
-            if (s, h, n0) not in results:
-                results[(s, h, n0)] = keep.tile([P, SIDE, end - n0], F32, name="result%d_%d_%d" % (s, h, n0))
-            col = ((s * SIDE + c) * M_TILES + h) * QUAD
+        def multiply(u):
+            window = slice(u * STEP, u * STEP + N)
+            for h in range(M_TILES):
+                for c in range(SIDE):
+                    rows = slice(c * ROWS, (c + 1) * ROWS)
+                    words = slice(FP4_WORD_BYTES * P * h, FP4_WORD_BYTES * P * (h + 1))
+                    nc.tensor.matmul_mx(
+                        out=bank(u, h, c)[:],
+                        lhsT=w_tiles[pair(u)][rows, words].bitcast(FP4X4),
+                        lhsT_scale=ws_tile[rows, pair(u), P * h : P * (h + 1)],
+                        rhs=codes[rows, window].bitcast(FP8X4),
+                        rhs_scale=scales[rows, window],
+                        start=True,
+                        stop=True,
+                    )
+
+        def read_out(u, h, c, on_vector):
+            col = ((pair(u) * SIDE + c) * M_TILES + h) * QUAD
             bias = bias_cols[:, col : col + 1]
-            sums = banks[(c, k)][:, N - (end - n0) :]
-            dst = results[(s, h, n0)][:, c, :]
+            sums = bank(u, h, c)[:, N - STEP :]
+            dst = results[(u, h)][:, c, :]
             if on_vector:
                 nc.vector.tensor_scalar(out=dst, in0=sums, scalar1=bias, scalar2=0.0, op0=ALU.add, op1=ALU.max)
             else:
                 nc.scalar.activation(out=dst, in_=sums, func=ACT.Relu, bias=bias)
 
-        def store(s, h, n0, end, c=None, queue=nc.sync):
-            if c is None:
-                queue.dma_start(out=out_view[s, h, :, :, n0:end], in_=results[(s, h, n0)][:])
-            else:
-                queue.dma_start(out=out_view[s, h, :, c, n0:end], in_=results[(s, h, n0)][:, c, :])
+        def finish(u):
+            for h in range(M_TILES):
+                tile = results[(u, h)]
+                target = out_view[pair(u), h, :, :, columns(u)]
+                for c in range(SIDE):
+                    read_out(u, h, c, c == 1 and u >= STEPS - SHARED_STEPS)
+                    if u == STEPS - 1:
+                        nc.sync.dma_start(out=target[:, c, :], in_=tile[:, c, :])
+                if u < STEPS - 1:
+                    nc.sync.dma_start(out=target, in_=tile[:])
 
-        def finish(s, h, n0, end, k, shared, apart=False):
-            read_out(False, s, h, 0, n0, end, k)
-            if apart:
-                store(s, h, n0, end, 0)
-            read_out(shared, s, h, 1, n0, end, k)
-            store(s, h, n0, end, 1 if apart else None)
+        load_weights(0)
+        load(0)
+        nc.vector.memset(ws_tile[:].bitcast(I32), 0)
+        nc.vector.memset(bias_rows[:], 0.0)
+        nc.vector.memset(codes[:, :STEP], 0)
+        nc.vector.memset(scales[:, :STEP].bitcast(I32), 0)
+        for r in range(SCALE_ROWS):
+            queue = nc.scalar if r % 2 else nc.sync
+            queue.dma_start(out=ws_tile[r:P:QUAD].bitcast(I32), in_=ws_view[r])
+        nc.scalar.dma_start(
+            out=bias_rows[0:P:QUAD, :].rearrange("q (j i) -> q j i", i=QUAD),
+            in_=b.rearrange("g (h q i) o -> q (g h) (i o)", h=M_TILES, i=QUAD),
+        )
+        for u in range(1, STEPS):
+            load(u)
+            if u == STEPS_PER_PAIR:
+                load_weights(1)
 
-        def load_weights():
-            nc.sync.dma_start(
-                out=w_tile[:].bitcast(I32),
-                in_=w_words.bitcast(I32).rearrange("(s c) p w -> (c p) s w", c=SIDE),
-            )
-
-        def zero():
-            nc.vector.memset(bias_rows[:], 0.0)
-            nc.vector.memset(ws_tile[:].bitcast(I32), 0)
-            nc.vector.memset(codes[:, :LEAD], 0)
-            nc.vector.memset(scales[:, :LEAD].bitcast(I32), 0)
-
-        def load_bias(queue):
-            queue.dma_start(
-                out=bias_rows[0:P:QUAD, :].rearrange("q (j i) -> q j i", i=QUAD),
-                in_=b.rearrange("g (h q i) o -> q (g h) (i o)", h=M_TILES, i=QUAD),
-            )
-
-        def load_scales(queue, mix=False):
-            ws_view = w_scales.bitcast(I32).rearrange("(s c) (k r) w -> r (c k) s w", c=SIDE, r=SCALE_ROWS)
-            for r in range(SCALE_ROWS):
-                (nc.gpsimd if mix and r == 0 else queue).dma_start(out=ws_tile[r:P:QUAD].bitcast(I32), in_=ws_view[r])
-
-        def turn_bias():
-            nc.vector.transpose(out=bias_cols[:], in_=bias_rows[:])
-
-        V, S = True, False
-        load_weights()
-        load(0, 0, 256)
-        zero()
-        load_bias(nc.scalar)
-        load_scales(nc.sync)
-        load(0, 256, 512)
-        load(1, 0, 256)
-        load(1, 256, 512)
-        interleave(V, 0, 0, 128)
-        interleave(V, 0, 128, 160)
-        interleave(S, 0, 160, 256)
-        quantize(0, 0, 128)
-        quantize(0, 128, 256)
-        multiply(0, 0, 256, 0)
-        turn_bias()
-        multiply(0, 1, 256, 1)
-        interleave(V, 0, 256, 384)
-        interleave(V, 0, 384, 448)
-        interleave(S, 0, 448, 512)
-        finish(0, 0, 0, 256, 0, False)
-        finish(0, 1, 0, 256, 1, False)
-        quantize(0, 256, 384)
-        quantize(0, 384, 512)
-        multiply(0, 0, 512, 2)
-        multiply(0, 1, 512, 3)
-        interleave(V, 1, 0, 128)
-        interleave(V, 1, 128, 256)
-        finish(0, 0, 256, 512, 2, False)
-        finish(0, 1, 256, 512, 3, False)
-        quantize(1, 0, 128)
-        quantize(1, 128, 256)
-        multiply(1, 0, 256, 0)
-        multiply(1, 1, 256, 1)
-        interleave(V, 1, 256, 384)
-        interleave(V, 1, 384, 512)
-        quantize(1, 256, 384)
-        quantize(1, 384, 512)
-        multiply(1, 0, 512, 2)
-        multiply(1, 1, 512, 3)
-        finish(1, 0, 0, 256, 0, True)
-        finish(1, 1, 0, 256, 1, True)
-        finish(1, 0, 256, 512, 2, True)
-        finish(1, 1, 256, 512, 3, True)
+        for u in range(STEPS):
+            interleave(u)
+            if 1 <= u <= STEPS - SHARED_STEPS:
+                finish(u - 1)
+            quantize(u)
+            if u == 0:
+                nc.vector.transpose(out=bias_cols[:], in_=bias_rows[:])
+            multiply(u)
+        for u in range(STEPS - SHARED_STEPS, STEPS):
+            finish(u)

@@ -139,8 +139,8 @@ def tile_rows_glin_relu_bias_kernel(tc, x, w_words, w_scales, b, out):
                 if u < STEPS - 1:
                     nc.sync.dma_start(out=target, in_=tile[:])
 
-        load_weights(0)
         load(0)
+        load_weights(0)
         nc.vector.memset(ws_tile[:].bitcast(I32), 0)
         nc.vector.memset(bias_rows[:], 0.0)
         nc.vector.memset(codes[:, :STEP], 0)
@@ -148,14 +148,14 @@ def tile_rows_glin_relu_bias_kernel(tc, x, w_words, w_scales, b, out):
         for r in range(SCALE_ROWS):
             queue = nc.scalar if r % 2 else nc.sync
             queue.dma_start(out=ws_tile[r:P:QUAD].bitcast(I32), in_=ws_view[r])
+        load(1)
+        load(2)
         nc.scalar.dma_start(
             out=bias_rows[0:P:QUAD, :].rearrange("q (j i) -> q j i", i=QUAD),
             in_=b.rearrange("g (h q i) o -> q (g h) (i o)", h=M_TILES, i=QUAD),
         )
-        for u in range(1, STEPS):
-            load(u)
-            if u == STEPS_PER_PAIR:
-                load_weights(1)
+        load_weights(1)
+        load(3)
 
         for u in range(STEPS):
             interleave(u)

@@ -23,6 +23,7 @@ PAIRS = G // SIDE
 M_TILES = M // P
 QUAD = 32
 SCALE_ROWS = 4
+BIAS_STEP = QUAD // (G * M_TILES)
 FP4_WORD_BYTES = 2
 STEP = 256
 STEPS_PER_PAIR = N // STEP
@@ -30,7 +31,7 @@ STEPS = PAIRS * STEPS_PER_PAIR
 PIECES = 2
 PIECE = STEP // PIECES
 RUN = 4
-SCALAR_COLS = ((40, 40), (0, 64), (0, 0), (0, 0))
+SCALAR_COLS = ((40, 40), (0, 64), (0, 0), (40, 40))
 SHARED_STEPS = 2
 
 
@@ -44,8 +45,8 @@ def tile_rows_glin_relu_bias_kernel(tc, x, w_words, w_scales, b, out):
 
         w_tiles = [keep.tile([P, FP4_WORD_BYTES * M], U8, name="w%d" % s, align_bytes=64) for s in range(PAIRS)]
         ws_tile = keep.tile([P, PAIRS, M], U8, align_bytes=64)
-        bias_rows = keep.tile([P, G * M_TILES * QUAD], F32, align_bytes=64)
-        bias_cols = keep.tile([P, G * M_TILES * QUAD], F32, align_bytes=64)
+        bias_rows = keep.tile([P, QUAD], F32, align_bytes=64)
+        bias_cols = keep.tile([P, QUAD], F32, align_bytes=64)
         codes = keep.tile([P, (STEPS + 1) * STEP], U32, align_bytes=64)
         scales = keep.tile([P, (STEPS + 1) * STEP], U8, align_bytes=64)
         grouped = [keep.tile([P, STEP, PACK], BF16, name="grouped%d" % u, align_bytes=64) for u in range(STEPS)]
@@ -119,7 +120,7 @@ def tile_rows_glin_relu_bias_kernel(tc, x, w_words, w_scales, b, out):
                     )
 
         def read_out(u, h, c, on_vector):
-            col = ((pair(u) * SIDE + c) * M_TILES + h) * QUAD
+            col = ((pair(u) * SIDE + c) * M_TILES + h) * BIAS_STEP
             bias = bias_cols[:, col : col + 1]
             sums = bank(u, h, c)[:, N - STEP :]
             dst = results[(u, h)][:, c, :]
@@ -151,7 +152,7 @@ def tile_rows_glin_relu_bias_kernel(tc, x, w_words, w_scales, b, out):
         load(1)
         load(2)
         nc.scalar.dma_start(
-            out=bias_rows[0:P:QUAD, :].rearrange("q (j i) -> q j i", i=QUAD),
+            out=bias_rows[0:P:BIAS_STEP, :],
             in_=b.rearrange("g (h q i) o -> q (g h) (i o)", h=M_TILES, i=QUAD),
         )
         load_weights(1)

@@ -31,8 +31,9 @@ STEPS = PAIRS * STEPS_PER_PAIR
 PIECES = 2
 PIECE = STEP // PIECES
 RUN = 4
-SCALAR_COLS = ((40, 40), (0, 64), (0, 0), (40, 40))
-SHARED_STEPS = 2
+SCALAR_COLS = ((0, 48), (0, 64), (0, 0), (0, 0))
+WHOLE = ((1, 1),)
+SHARED_STEPS = 1
 
 
 def tile_rows_glin_relu_bias_kernel(tc, x, w_words, w_scales, b, out):
@@ -50,10 +51,22 @@ def tile_rows_glin_relu_bias_kernel(tc, x, w_words, w_scales, b, out):
         codes = keep.tile([P, (STEPS + 1) * STEP], U32, align_bytes=64)
         scales = keep.tile([P, (STEPS + 1) * STEP], U8, align_bytes=64)
         grouped = [keep.tile([P, STEP, PACK], BF16, name="grouped%d" % u, align_bytes=64) for u in range(STEPS)]
+
+        def pair(u):
+            return u // STEPS_PER_PAIR
+
+        def width(u, h):
+            if (pair(u), h) not in WHOLE:
+                return STEP
+            return N if u % STEPS_PER_PAIR == STEPS_PER_PAIR - 1 else 0
+
+        def tiles(u):
+            return [h for h in range(M_TILES) if width(u, h)]
+
         results = {
-            (u, h): keep.tile([P, SIDE, STEP], F32, name="result%d_%d" % (u, h))
+            (u, h): keep.tile([P, SIDE, width(u, h)], F32, name="result%d_%d" % (u, h))
             for u in range(STEPS)
-            for h in range(M_TILES)
+            for h in tiles(u)
         }
         banks = {
             (c, k): psum.tile([P, N], F32, name="bank%d_%d" % (c, k))
@@ -66,9 +79,6 @@ def tile_rows_glin_relu_bias_kernel(tc, x, w_words, w_scales, b, out):
         w_view = w_words.bitcast(I32).rearrange("(s c) p w -> s (c p) w", c=SIDE)
         ws_view = w_scales.bitcast(I32).rearrange("(s c) (k r) w -> r (c k) s w", c=SIDE, r=SCALE_ROWS)
         raw = {}
-
-        def pair(u):
-            return u // STEPS_PER_PAIR
 
         def columns(u):
             n0 = (u % STEPS_PER_PAIR) * STEP
@@ -105,7 +115,7 @@ def tile_rows_glin_relu_bias_kernel(tc, x, w_words, w_scales, b, out):
 
         def multiply(u):
             window = slice(u * STEP, u * STEP + N)
-            for h in range(M_TILES):
+            for h in tiles(u):
                 for c in range(SIDE):
                     rows = slice(c * ROWS, (c + 1) * ROWS)
                     words = slice(FP4_WORD_BYTES * P * h, FP4_WORD_BYTES * P * (h + 1))
@@ -122,7 +132,7 @@ def tile_rows_glin_relu_bias_kernel(tc, x, w_words, w_scales, b, out):
         def read_out(u, h, c, on_vector):
             col = ((pair(u) * SIDE + c) * M_TILES + h) * BIAS_STEP
             bias = bias_cols[:, col : col + 1]
-            sums = bank(u, h, c)[:, N - STEP :]
+            sums = bank(u, h, c)[:, N - width(u, h) :]
             dst = results[(u, h)][:, c, :]
             if on_vector:
                 nc.vector.tensor_scalar(out=dst, in0=sums, scalar1=bias, scalar2=0.0, op0=ALU.add, op1=ALU.max)
@@ -130,14 +140,15 @@ def tile_rows_glin_relu_bias_kernel(tc, x, w_words, w_scales, b, out):
                 nc.scalar.activation(out=dst, in_=sums, func=ACT.Relu, bias=bias)
 
         def finish(u):
-            for h in range(M_TILES):
+            for h in tiles(u):
                 tile = results[(u, h)]
-                target = out_view[pair(u), h, :, :, columns(u)]
+                end = columns(u).stop
+                target = out_view[pair(u), h, :, :, end - width(u, h) : end]
                 for c in range(SIDE):
                     read_out(u, h, c, c == 1 and u >= STEPS - SHARED_STEPS)
-                    if u == STEPS - 1:
+                    if u in (0, STEPS - 1):
                         nc.sync.dma_start(out=target[:, c, :], in_=tile[:, c, :])
-                if u < STEPS - 1:
+                if u not in (0, STEPS - 1):
                     nc.sync.dma_start(out=target, in_=tile[:])
 
         load(0)

@@ -32,8 +32,8 @@ PIECES = 2
 PIECE = STEP // PIECES
 RUN = 4
 SCALAR_COLS = ((0, 48), (0, 64), (0, 0), (0, 0))
-WHOLE = ((1, 1),)
 SHARED_STEPS = 1
+EARLY_GROUPS = 1
 
 
 def tile_rows_glin_relu_bias_kernel(tc, x, w_words, w_scales, b, out):
@@ -55,18 +55,18 @@ def tile_rows_glin_relu_bias_kernel(tc, x, w_words, w_scales, b, out):
         def pair(u):
             return u // STEPS_PER_PAIR
 
-        def width(u, h):
-            if (pair(u), h) not in WHOLE:
+        def width(u, h, c):
+            if h == 0 or pair(u) * SIDE + c < EARLY_GROUPS:
                 return STEP
             return N if u % STEPS_PER_PAIR == STEPS_PER_PAIR - 1 else 0
 
-        def tiles(u):
-            return [h for h in range(M_TILES) if width(u, h)]
+        def passes(u):
+            return [(h, c) for h in range(M_TILES) for c in range(SIDE) if width(u, h, c)]
 
         results = {
-            (u, h): keep.tile([P, SIDE, width(u, h)], F32, name="result%d_%d" % (u, h))
+            (u, h, c): keep.tile([P, width(u, h, c)], F32, name="result%d_%d_%d" % (u, h, c))
             for u in range(STEPS)
-            for h in tiles(u)
+            for h, c in passes(u)
         }
         banks = {
             (c, k): psum.tile([P, N], F32, name="bank%d_%d" % (c, k))
@@ -115,41 +115,31 @@ def tile_rows_glin_relu_bias_kernel(tc, x, w_words, w_scales, b, out):
 
         def multiply(u):
             window = slice(u * STEP, u * STEP + N)
-            for h in tiles(u):
-                for c in range(SIDE):
-                    rows = slice(c * ROWS, (c + 1) * ROWS)
-                    words = slice(FP4_WORD_BYTES * P * h, FP4_WORD_BYTES * P * (h + 1))
-                    nc.tensor.matmul_mx(
-                        out=bank(u, h, c)[:],
-                        lhsT=w_tiles[pair(u)][rows, words].bitcast(FP4X4),
-                        lhsT_scale=ws_tile[rows, pair(u), P * h : P * (h + 1)],
-                        rhs=codes[rows, window].bitcast(FP8X4),
-                        rhs_scale=scales[rows, window],
-                        start=True,
-                        stop=True,
-                    )
-
-        def read_out(u, h, c, on_vector):
-            col = ((pair(u) * SIDE + c) * M_TILES + h) * BIAS_STEP
-            bias = bias_cols[:, col : col + 1]
-            sums = bank(u, h, c)[:, N - width(u, h) :]
-            dst = results[(u, h)][:, c, :]
-            if on_vector:
-                nc.vector.tensor_scalar(out=dst, in0=sums, scalar1=bias, scalar2=0.0, op0=ALU.add, op1=ALU.max)
-            else:
-                nc.scalar.activation(out=dst, in_=sums, func=ACT.Relu, bias=bias)
+            for h, c in passes(u):
+                rows = slice(c * ROWS, (c + 1) * ROWS)
+                words = slice(FP4_WORD_BYTES * P * h, FP4_WORD_BYTES * P * (h + 1))
+                nc.tensor.matmul_mx(
+                    out=bank(u, h, c)[:],
+                    lhsT=w_tiles[pair(u)][rows, words].bitcast(FP4X4),
+                    lhsT_scale=ws_tile[rows, pair(u), P * h : P * (h + 1)],
+                    rhs=codes[rows, window].bitcast(FP8X4),
+                    rhs_scale=scales[rows, window],
+                    start=True,
+                    stop=True,
+                )
 
         def finish(u):
-            for h in tiles(u):
-                tile = results[(u, h)]
-                end = columns(u).stop
-                target = out_view[pair(u), h, :, :, end - width(u, h) : end]
-                for c in range(SIDE):
-                    read_out(u, h, c, c == 1 and u >= STEPS - SHARED_STEPS)
-                    if u in (0, STEPS - 1):
-                        nc.sync.dma_start(out=target[:, c, :], in_=tile[:, c, :])
-                if u not in (0, STEPS - 1):
-                    nc.sync.dma_start(out=target, in_=tile[:])
+            end = columns(u).stop
+            for h, c in passes(u):
+                col = ((pair(u) * SIDE + c) * M_TILES + h) * BIAS_STEP
+                bias = bias_cols[:, col : col + 1]
+                sums = bank(u, h, c)[:, N - width(u, h, c) :]
+                dst = results[(u, h, c)][:]
+                if c == 1 and u >= STEPS - SHARED_STEPS:
+                    nc.vector.tensor_scalar(out=dst, in0=sums, scalar1=bias, scalar2=0.0, op0=ALU.add, op1=ALU.max)
+                else:
+                    nc.scalar.activation(out=dst, in_=sums, func=ACT.Relu, bias=bias)
+                nc.sync.dma_start(out=out_view[pair(u), h, :, c, end - width(u, h, c) : end], in_=dst)
 
         load(0)
         load_weights(0)
@@ -166,8 +156,8 @@ def tile_rows_glin_relu_bias_kernel(tc, x, w_words, w_scales, b, out):
             out=bias_rows[0:P:BIAS_STEP, :],
             in_=b.rearrange("g (h q i) o -> q (g h) (i o)", h=M_TILES, i=QUAD),
         )
-        load_weights(1)
         load(3)
+        load_weights(1)
 
         for u in range(STEPS):
             interleave(u)

@@ -25,6 +25,7 @@ QUAD = 32
 SCALE_ROWS = 4
 BIAS_STEP = QUAD // (G * M_TILES)
 FP4_WORD_BYTES = 2
+DMA_ALIGN = 256
 STEP = 256
 STEPS_PER_PAIR = N // STEP
 STEPS = PAIRS * STEPS_PER_PAIR
@@ -44,9 +45,9 @@ def tile_rows_glin_relu_bias_kernel(tc, x, w_words, w_scales, b, out):
         psum = ctx.enter_context(tc.psum_pool(name="psum", bufs=1))
         ctx.enter_context(tc.manual_schedule())
 
-        w_tiles = [keep.tile([P, FP4_WORD_BYTES * M], U8, name="w%d" % s, align_bytes=64) for s in range(PAIRS)]
-        ws_tile = keep.tile([P, PAIRS, M], U8, align_bytes=64)
-        bias_rows = keep.tile([P, QUAD], F32, align_bytes=64)
+        w_tiles = [keep.tile([P, FP4_WORD_BYTES * M], U8, name="w%d" % s, align_bytes=DMA_ALIGN) for s in range(PAIRS)]
+        ws_tile = keep.tile([P, PAIRS, M], U8, align_bytes=DMA_ALIGN)
+        bias_rows = keep.tile([P, QUAD], F32, align_bytes=DMA_ALIGN)
         bias_cols = keep.tile([P, QUAD], F32, align_bytes=64)
         codes = keep.tile([P, (STEPS + 1) * STEP], U32, align_bytes=64)
         scales = keep.tile([P, (STEPS + 1) * STEP], U8, align_bytes=64)
@@ -64,7 +65,7 @@ def tile_rows_glin_relu_bias_kernel(tc, x, w_words, w_scales, b, out):
             return [(h, c) for h in range(M_TILES) for c in range(SIDE) if width(u, h, c)]
 
         results = {
-            (u, h, c): keep.tile([P, width(u, h, c)], F32, name="result%d_%d_%d" % (u, h, c))
+            (u, h, c): keep.tile([P, width(u, h, c)], F32, name="result%d_%d_%d" % (u, h, c), align_bytes=DMA_ALIGN)
             for u in range(STEPS)
             for h, c in passes(u)
         }
@@ -88,7 +89,7 @@ def tile_rows_glin_relu_bias_kernel(tc, x, w_words, w_scales, b, out):
             return banks[(c, (u % 2) * M_TILES + h)]
 
         def load(u):
-            raw[u] = raw_pool.tile([P, PACK, STEP], F32, name="raw")
+            raw[u] = raw_pool.tile([P, PACK, STEP], F32, name="raw", align_bytes=DMA_ALIGN)
             nc.sync.dma_start(out=raw[u][:], in_=x_view[pair(u), :, :, columns(u)])
 
         def load_weights(s):

@@ -33,8 +33,7 @@ PIECES = 2
 PIECE = STEP // PIECES
 RUN = 4
 SCALAR_COLS = ((0, 48), (0, 64), (0, 0), (0, 0))
-SHARED_STEPS = 1
-EARLY_GROUPS = 1
+LAST = STEPS - 1
 
 
 def tile_rows_glin_relu_bias_kernel(tc, x, w_words, w_scales, b, out):
@@ -56,19 +55,10 @@ def tile_rows_glin_relu_bias_kernel(tc, x, w_words, w_scales, b, out):
         def pair(u):
             return u // STEPS_PER_PAIR
 
-        def width(u, h, c):
-            if h == 0 or pair(u) * SIDE + c < EARLY_GROUPS:
-                return STEP
-            return N if u % STEPS_PER_PAIR == STEPS_PER_PAIR - 1 else 0
-
-        def passes(u):
-            return [(h, c) for h in range(M_TILES) for c in range(SIDE) if width(u, h, c)]
-
-        results = {
-            (u, h, c): keep.tile([P, width(u, h, c)], F32, name="result%d_%d_%d" % (u, h, c), align_bytes=DMA_ALIGN)
-            for u in range(STEPS)
-            for h, c in passes(u)
-        }
+        passes = [(h, c) for h in range(M_TILES) for c in range(SIDE)]
+        results = [
+            keep.tile([P, M_TILES, SIDE, STEP], F32, name="result%d" % u, align_bytes=DMA_ALIGN) for u in range(STEPS)
+        ]
         banks = {
             (c, k): psum.tile([P, N], F32, name="bank%d_%d" % (c, k))
             for c in range(SIDE)
@@ -116,7 +106,7 @@ def tile_rows_glin_relu_bias_kernel(tc, x, w_words, w_scales, b, out):
 
         def multiply(u):
             window = slice(u * STEP, u * STEP + N)
-            for h, c in passes(u):
+            for h, c in passes:
                 rows = slice(c * ROWS, (c + 1) * ROWS)
                 words = slice(FP4_WORD_BYTES * P * h, FP4_WORD_BYTES * P * (h + 1))
                 nc.tensor.matmul_mx(
@@ -130,17 +120,18 @@ def tile_rows_glin_relu_bias_kernel(tc, x, w_words, w_scales, b, out):
                 )
 
         def finish(u):
-            end = columns(u).stop
-            for h, c in passes(u):
+            for h, c in passes:
                 col = ((pair(u) * SIDE + c) * M_TILES + h) * BIAS_STEP
                 bias = bias_cols[:, col : col + 1]
-                sums = bank(u, h, c)[:, N - width(u, h, c) :]
-                dst = results[(u, h, c)][:]
-                if c == 1 and u >= STEPS - SHARED_STEPS:
+                sums = bank(u, h, c)[:, N - STEP :]
+                dst = results[u][:, h, c]
+                if c == 1 and u == LAST:
                     nc.vector.tensor_scalar(out=dst, in0=sums, scalar1=bias, scalar2=0.0, op0=ALU.add, op1=ALU.max)
+                    nc.sync.dma_start(out=out_view[pair(u), h, :, :, columns(u)], in_=results[u][:, h])
                 else:
                     nc.scalar.activation(out=dst, in_=sums, func=ACT.Relu, bias=bias)
-                nc.sync.dma_start(out=out_view[pair(u), h, :, c, end - width(u, h, c) : end], in_=dst)
+                    if u != LAST:
+                        nc.sync.dma_start(out=out_view[pair(u), h, :, c, columns(u)], in_=dst)
 
         load(0)
         load_weights(0)
@@ -149,24 +140,21 @@ def tile_rows_glin_relu_bias_kernel(tc, x, w_words, w_scales, b, out):
         nc.vector.memset(codes[:, :STEP], 0)
         nc.vector.memset(scales[:, :STEP].bitcast(I32), 0)
         for r in range(SCALE_ROWS):
-            queue = nc.scalar if r % 2 else nc.sync
-            queue.dma_start(out=ws_tile[r:P:QUAD].bitcast(I32), in_=ws_view[r])
-        load(1)
-        load(2)
-        nc.scalar.dma_start(
+            nc.sync.dma_start(out=ws_tile[r:P:QUAD].bitcast(I32), in_=ws_view[r])
+        nc.sync.dma_start(
             out=bias_rows[0:P:BIAS_STEP, :],
             in_=b.rearrange("g (h q i) o -> q (g h) (i o)", h=M_TILES, i=QUAD),
         )
-        load(3)
+        for u in range(1, STEPS):
+            load(u)
         load_weights(1)
 
         for u in range(STEPS):
             interleave(u)
-            if 1 <= u <= STEPS - SHARED_STEPS:
+            if u >= 1:
                 finish(u - 1)
             quantize(u)
             if u == 0:
                 nc.vector.transpose(out=bias_cols[:], in_=bias_rows[:])
             multiply(u)
-        for u in range(STEPS - SHARED_STEPS, STEPS):
-            finish(u)
+        finish(LAST)

@@ -119,19 +119,21 @@ def tile_rows_glin_relu_bias_kernel(tc, x, w_words, w_scales, b, out):
                     stop=True,
                 )
 
+        def read(u, h, c, on_vector):
+            col = ((pair(u) * SIDE + c) * M_TILES + h) * BIAS_STEP
+            bias = bias_cols[:, col : col + 1]
+            sums = bank(u, h, c)[:, N - STEP :]
+            dst = results[u][:, h, c]
+            if on_vector:
+                nc.vector.tensor_scalar(out=dst, in0=sums, scalar1=bias, scalar2=0.0, op0=ALU.add, op1=ALU.max)
+            else:
+                nc.scalar.activation(out=dst, in_=sums, func=ACT.Relu, bias=bias)
+            nc.sync.dma_start(out=out_view[pair(u), h, :, c, columns(u)], in_=dst)
+
         def finish(u):
-            for h, c in passes:
-                col = ((pair(u) * SIDE + c) * M_TILES + h) * BIAS_STEP
-                bias = bias_cols[:, col : col + 1]
-                sums = bank(u, h, c)[:, N - STEP :]
-                dst = results[u][:, h, c]
-                if c == 1 and u == LAST:
-                    nc.vector.tensor_scalar(out=dst, in0=sums, scalar1=bias, scalar2=0.0, op0=ALU.add, op1=ALU.max)
-                    nc.sync.dma_start(out=out_view[pair(u), h, :, :, columns(u)], in_=results[u][:, h])
-                else:
-                    nc.scalar.activation(out=dst, in_=sums, func=ACT.Relu, bias=bias)
-                    if u != LAST:
-                        nc.sync.dma_start(out=out_view[pair(u), h, :, c, columns(u)], in_=dst)
+            for h in range(M_TILES):
+                for c in range(SIDE):
+                    read(u, h, c, on_vector=pair(u) == 1 and c == 1)
 
         load(0)
         load_weights(0)
@@ -151,10 +153,12 @@ def tile_rows_glin_relu_bias_kernel(tc, x, w_words, w_scales, b, out):
 
         for u in range(STEPS):
             interleave(u)
-            if u >= 1:
+            if 1 <= u <= STEPS_PER_PAIR:
                 finish(u - 1)
             quantize(u)
             if u == 0:
                 nc.vector.transpose(out=bias_cols[:], in_=bias_rows[:])
+            if u == LAST:
+                finish(u - 1)
             multiply(u)
         finish(LAST)

@@ -34,6 +34,8 @@ PIECE = STEP // PIECES
 RUN = 4
 SCALAR_COLS = ((0, 48), (0, 64), (0, 0), (0, 0))
 LAST = STEPS - 1
+SINGLY = ((0, 1), (2, 3), (1, 2), (3, 4))
+STORES = (SINGLY, SINGLY, ((0, 1), (2, 3), (1, 4, 2)), ((0, 4, 2), (1, 4, 2)))
 
 
 def tile_rows_glin_relu_bias_kernel(tc, x, w_words, w_scales, b, out):
@@ -57,7 +59,7 @@ def tile_rows_glin_relu_bias_kernel(tc, x, w_words, w_scales, b, out):
 
         passes = [(h, c) for h in range(M_TILES) for c in range(SIDE)]
         results = [
-            keep.tile([P, M_TILES, SIDE, STEP], F32, name="result%d" % u, align_bytes=DMA_ALIGN) for u in range(STEPS)
+            keep.tile([P, SIDE * M_TILES, STEP], F32, name="result%d" % u, align_bytes=DMA_ALIGN) for u in range(STEPS)
         ]
         banks = {
             (c, k): psum.tile([P, N], F32, name="bank%d_%d" % (c, k))
@@ -66,7 +68,7 @@ def tile_rows_glin_relu_bias_kernel(tc, x, w_words, w_scales, b, out):
         }
 
         x_view = x.rearrange("(s c) (p t) n -> s (c p) t n", c=SIDE, t=PACK)
-        out_view = out.rearrange("(s c) (h m) n -> s h m c n", c=SIDE, m=P)
+        out_view = out.rearrange("(s c) (h m) n -> s m (c h) n", c=SIDE, m=P)
         w_view = w_words.bitcast(I32).rearrange("(s c) p w -> s (c p) w", c=SIDE)
         ws_view = w_scales.bitcast(I32).rearrange("(s c) (k r) w -> r (c k) s w", c=SIDE, r=SCALE_ROWS)
         raw = {}
@@ -123,17 +125,21 @@ def tile_rows_glin_relu_bias_kernel(tc, x, w_words, w_scales, b, out):
             col = ((pair(u) * SIDE + c) * M_TILES + h) * BIAS_STEP
             bias = bias_cols[:, col : col + 1]
             sums = bank(u, h, c)[:, N - STEP :]
-            dst = results[u][:, h, c]
+            dst = results[u][:, c * M_TILES + h]
             if on_vector:
                 nc.vector.tensor_scalar(out=dst, in0=sums, scalar1=bias, scalar2=0.0, op0=ALU.add, op1=ALU.max)
             else:
                 nc.scalar.activation(out=dst, in_=sums, func=ACT.Relu, bias=bias)
-            nc.sync.dma_start(out=out_view[pair(u), h, :, c, columns(u)], in_=dst)
+
+        def store(u, tiles):
+            nc.sync.dma_start(out=out_view[pair(u), :, tiles, columns(u)], in_=results[u][:, tiles])
 
         def finish(u):
             for h in range(M_TILES):
                 for c in range(SIDE):
                     read(u, h, c, on_vector=pair(u) == 1 and c == 1)
+            for tiles in STORES[u]:
+                store(u, slice(*tiles))
 
         load(0)
         load_weights(0)

@@ -148,7 +148,8 @@ def tile_rows_glin_relu_bias_kernel(tc, x, w_words, w_scales, b, out):
         nc.vector.memset(codes[:, :STEP], 0)
         nc.vector.memset(scales[:, :STEP].bitcast(I32), 0)
         for r in range(SCALE_ROWS):
-            nc.sync.dma_start(out=ws_tile[r:P:QUAD].bitcast(I32), in_=ws_view[r])
+            queue = nc.scalar if r < SCALE_ROWS // 2 else nc.sync
+            queue.dma_start(out=ws_tile[r:P:QUAD].bitcast(I32), in_=ws_view[r])
         nc.sync.dma_start(
             out=bias_rows[0:P:BIAS_STEP, :],
             in_=b.rearrange("g (h q i) o -> q (g h) (i o)", h=M_TILES, i=QUAD),

from contextlib import ExitStack

import concourse.mybir as mybir

G, D, M, N = 4, 256, 256, 512
FLOPS = 2 * G * D * M * N

F32 = mybir.dt.float32
BF16 = mybir.dt.bfloat16
I32 = mybir.dt.int32
U32 = mybir.dt.uint32
U8 = mybir.dt.uint8
FP8X4 = mybir.dt.float8_e4m3fn_x4
FP4X4 = mybir.dt.float4_e2m1fn_x4
ACT = mybir.ActivationFunctionType
ALU = mybir.AluOpType

P = 128
PACK = 4
ROWS = D // PACK
SIDE = P // ROWS
PAIRS = G // SIDE
M_TILES = M // P
QUAD = 32
SCALE_ROWS = 4
BIAS_STEP = QUAD // (G * M_TILES)
FP4_WORD_BYTES = 2
DMA_ALIGN = 256
STEP = 256
STEPS_PER_PAIR = N // STEP
STEPS = PAIRS * STEPS_PER_PAIR
PIECES = 2
PIECE = STEP // PIECES
RUN = 4
SCALAR_COLS = ((0, 48), (0, 64), (0, 0), (0, 0))
LAST = STEPS - 1
SINGLY = ((0, 1), (2, 3), (1, 2), (3, 4))
STORES = (SINGLY, SINGLY, ((0, 1), (2, 3), (1, 4, 2)), ((0, 4, 2), (1, 4, 2)))


def tile_rows_glin_relu_bias_kernel(tc, x, w_words, w_scales, b, out):
    nc = tc.nc
    with ExitStack() as ctx:
        keep = ctx.enter_context(tc.tile_pool(name="keep", bufs=1))
        raw_pool = ctx.enter_context(tc.tile_pool(name="raw", bufs=STEPS))
        psum = ctx.enter_context(tc.psum_pool(name="psum", bufs=1))
        ctx.enter_context(tc.manual_schedule())

        w_tiles = [keep.tile([P, FP4_WORD_BYTES * M], U8, name="w%d" % s, align_bytes=DMA_ALIGN) for s in range(PAIRS)]
        ws_tile = keep.tile([P, PAIRS, M], U8, align_bytes=DMA_ALIGN)
        bias_rows = keep.tile([P, QUAD], F32, align_bytes=DMA_ALIGN)
        bias_cols = keep.tile([P, QUAD], F32, align_bytes=64)
        codes = keep.tile([P, (STEPS + 1) * STEP], U32, align_bytes=64)
        scales = keep.tile([P, (STEPS + 1) * STEP], U8, align_bytes=64)
        grouped = [keep.tile([P, STEP, PACK], BF16, name="grouped%d" % u, align_bytes=64) for u in range(STEPS)]

        def pair(u):
            return u // STEPS_PER_PAIR

        passes = [(h, c) for h in range(M_TILES) for c in range(SIDE)]
        results = [
            keep.tile([P, SIDE * M_TILES, STEP], F32, name="result%d" % u, align_bytes=DMA_ALIGN) for u in range(STEPS)
        ]
        banks = {
            (c, k): psum.tile([P, N], F32, name="bank%d_%d" % (c, k))
            for c in range(SIDE)
            for k in range(2 * M_TILES)
        }

        x_view = x.rearrange("(s c) (p t) n -> s (c p) t n", c=SIDE, t=PACK)
        out_view = out.rearrange("(s c) (h m) n -> s m (c h) n", c=SIDE, m=P)
        w_view = w_words.bitcast(I32).rearrange("(s c) p w -> s (c p) w", c=SIDE)
        ws_view = w_scales.bitcast(I32).rearrange("(s c) (k r) w -> r (c k) s w", c=SIDE, r=SCALE_ROWS)
        raw = {}

        def columns(u):
            n0 = (u % STEPS_PER_PAIR) * STEP
            return slice(n0, n0 + STEP)

        def bank(u, h, c):
            return banks[(c, (u % 2) * M_TILES + h)]

        def load(u):
            raw[u] = raw_pool.tile([P, PACK, STEP], F32, name="raw", align_bytes=DMA_ALIGN)
            nc.sync.dma_start(out=raw[u][:], in_=x_view[pair(u), :, :, columns(u)])

        def load_weights(s):
            nc.sync.dma_start(out=w_tiles[s][:].bitcast(I32), in_=w_view[s])

        def interleave(u):
            src = raw[u][:].rearrange("p t (r i) -> p r t i", i=RUN)
            dst = grouped[u][:].rearrange("p (r i) t -> p r t i", i=RUN)
            for j, scalar_cols in enumerate(SCALAR_COLS[u]):
                start, end = j * PIECE // RUN, (j + 1) * PIECE // RUN
                cut = end - scalar_cols // RUN
                nc.vector.tensor_copy(out=dst[:, start:cut], in_=src[:, start:cut])
                if scalar_cols:
                    nc.scalar.copy(out=dst[:, cut:end], in_=src[:, cut:end])

        def quantize(u):
            for n0 in range(0, STEP, PIECE):
                cols = slice((u + 1) * STEP + n0, (u + 1) * STEP + n0 + PIECE)
                nc.vector.quantize_mx(
                    out=codes[:, cols].bitcast(FP8X4),
                    scales=scales[:, cols],
                    in_=grouped[u][:, n0 : n0 + PIECE, :].rearrange("p n t -> p (n t)"),
                )

        def multiply(u):
            window = slice(u * STEP, u * STEP + N)
            for h, c in passes:
                rows = slice(c * ROWS, (c + 1) * ROWS)
                words = slice(FP4_WORD_BYTES * P * h, FP4_WORD_BYTES * P * (h + 1))
                nc.tensor.matmul_mx(
                    out=bank(u, h, c)[:],
                    lhsT=w_tiles[pair(u)][rows, words].bitcast(FP4X4),
                    lhsT_scale=ws_tile[rows, pair(u), P * h : P * (h + 1)],
                    rhs=codes[rows, window].bitcast(FP8X4),
                    rhs_scale=scales[rows, window],
                    start=True,
                    stop=True,
                )

        def read(u, h, c, on_vector):
            col = ((pair(u) * SIDE + c) * M_TILES + h) * BIAS_STEP
            bias = bias_cols[:, col : col + 1]
            sums = bank(u, h, c)[:, N - STEP :]
            dst = results[u][:, c * M_TILES + h]
            if on_vector:
                nc.vector.tensor_scalar(out=dst, in0=sums, scalar1=bias, scalar2=0.0, op0=ALU.add, op1=ALU.max)
            else:
                nc.scalar.activation(out=dst, in_=sums, func=ACT.Relu, bias=bias)

        def store(u, tiles):
            nc.sync.dma_start(out=out_view[pair(u), :, tiles, columns(u)], in_=results[u][:, tiles])

        def finish(u):
            for h in range(M_TILES):
                for c in range(SIDE):
                    read(u, h, c, on_vector=pair(u) == 1 and c == 1)
            for tiles in STORES[u]:
                store(u, slice(*tiles))

        load(0)
        load_weights(0)
        nc.vector.memset(ws_tile[:].bitcast(I32), 0)
        nc.vector.memset(bias_rows[:], 0.0)
        nc.vector.memset(codes[:, :STEP], 0)
        nc.vector.memset(scales[:, :STEP].bitcast(I32), 0)
        for r in range(SCALE_ROWS):
            queue = nc.scalar if r < SCALE_ROWS // 2 else nc.sync
            queue.dma_start(out=ws_tile[r:P:QUAD].bitcast(I32), in_=ws_view[r])
        nc.sync.dma_start(
            out=bias_rows[0:P:BIAS_STEP, :],
            in_=b.rearrange("g (h q i) o -> q (g h) (i o)", h=M_TILES, i=QUAD),
        )
        for u in range(1, STEPS):
            load(u)
        load_weights(1)

        for u in range(STEPS):
            interleave(u)
            if 1 <= u <= STEPS_PER_PAIR:
                finish(u - 1)
            quantize(u)
            if u == 0:
                nc.vector.transpose(out=bias_cols[:], in_=bias_rows[:])
            if u == LAST:
                finish(u - 1)
            multiply(u)
        finish(LAST)
